import numpy as np, ml_dtypes
CORES = [10,34,74,98]
N = 4
import mx_ref
BF = ml_dtypes.bfloat16
def gentries(a):
    return np.ascontiguousarray(a.reshape(8, 16, -1).transpose(0, 2, 1)).reshape(8, -1)
def gtable(e):
    e = np.asarray(e); return np.ascontiguousarray(e.reshape(8, -1, 16).transpose(0, 2, 1)).reshape(128, -1).astype(np.int32)
def gcols(t, e):
    v = np.concatenate([t.reshape(8, 16, -1, 4), np.zeros((8, 16, 1, 4), BF)], axis=2)
    return np.ascontiguousarray(np.stack([v[g][:, e[g]] for g in range(8)])).reshape(128, -1)
def cols(t, e):
    v = np.concatenate([t.reshape(128, -1, 4), np.zeros((128, 1, 4), BF)], axis=1)
    return np.ascontiguousarray(v[:, e]).reshape(128, -1)
def tile(rs):
    return np.stack(rs, axis=2).reshape(128, -1).astype(BF)
def pick(q, e):
    c = np.concatenate([q[0].reshape(128, -1, 4), np.zeros((128, 1, 4), np.uint8)], axis=1); s = np.concatenate([q[1], np.ones((16, 1), np.uint8)], axis=1)
    return (np.ascontiguousarray(c[:, e].reshape(128, -1)), np.ascontiguousarray(s[:, e]))
def join(*qs):
    return (np.concatenate([q[0] for q in qs], axis=1), np.concatenate([q[1] for q in qs], axis=1))
def put(q, e, v):
    c, s = q[0].reshape(128, -1, 4).copy(), q[1].copy(); c[:, e] = v[0].reshape(128, -1, 4); s[:, e] = v[1]
    return (c.reshape(128, -1), s)
def pk(c, s):
    return (np.ascontiguousarray(c), mx_ref.live(s))
def emit(q):
    return q[0], q[1]
def packed(v, rng):
    q = [mx_ref.quantize(np.ascontiguousarray(v[r])) for r in range(N)]
    return np.stack([a for a, b in q]), np.stack([mx_ref.plane(b, rng) for a, b in q])
def values_of_codes():
    e, c = np.zeros((128, 128, 4), np.float32), np.zeros((128, 2, 4), np.uint8)
    e[np.arange(128), np.arange(128), 0] = 1
    c[:127, :, 0] = np.arange(256).reshape(2, 128).T[:127]
    return mx_ref.matmul(mx_ref.quantize(e.reshape(128, 512).astype(BF)), (c.reshape(128, 8), np.full((16, 2), 127, np.uint8))).T.reshape(-1).astype(np.float64)
CODE_VALUE, SCALE_VALUE = values_of_codes(), 2.0 ** (np.arange(256) - 127.0)
def decode(q):
    return (CODE_VALUE[q[0]].reshape(16, 8, -1, 4) * SCALE_VALUE[q[1]][:, None, :, None] + 0.0).reshape(128, -1).astype(np.float32)
def f(rng, *shape):
    return mx_ref.flush((rng.standard_normal(shape, dtype=np.float32) * np.exp2(rng.integers(-2, 3, shape[:-1] + (1,)))).astype(BF))
def wide(rng, *shape, cols=0):
    v = rng.standard_normal(shape, dtype=np.float32) * np.exp2(rng.integers(-12, 13, shape)).astype(np.float32)
    if cols: v *= np.repeat(np.exp2(rng.integers(-cols, cols + 1, shape[:-2] + (1, shape[-1] // 4))) * (rng.random(shape[:-2] + (1, shape[-1] // 4)) > 0.0625), 4, axis=-1).astype(np.float32)
    return mx_ref.flush(v.astype(BF))
C, J, K, R = 288, 448, 160, 3
def big(v):
    v = v.astype(np.float32)
    v[np.abs(v) < np.float32(2.0 ** -16)] = 0
    return v.astype(BF)
def numbers_of(rng):
    return {"x": big(f(rng, N, 128, 4 * C)), "u": np.array(f(rng, N, 128, 512)), "v": np.array(f(rng, N, 128, 512))}
def paths(rng, n):
    a = np.zeros((8, J), np.int64)
    a[0] = rng.integers(0, C, J)
    for g in range(1, 8):
        a[g] = np.where(rng.random(J) < 0.5, a[g - 1], n[rng.integers(0, 8, J), a[g - 1]])
    return a
def lists(rng):
    n = rng.integers(0, C, (8, C))
    return {"nb": np.stack([gtable(n)] * N), "p": np.stack([gtable(paths(rng, n)) for r in range(N)])}
def weights(rng, kept=[]):
    w = (rng.random((N, 128, 512, 4), dtype=np.float32) * 2 - 1) * np.float32(2.0 ** -6)
    for i in range(2):
        k = rng.integers(0, 512, (N, 512))
        w[np.arange(N)[:, None], k >> 2, np.arange(512)[None], k & 3] = (3 + 6 * rng.random((N, 512))) * rng.choice([-1.0, 1.0], (N, 512))
    w = w.reshape(N, 128, 4, 128, 4)
    for i in kept:
        for h in range(i, 128, 16):
            w[:, :, :, h] = 0
            for b in range(4): w[:, h, b, h, b] = 32
    c, s = packed(w.reshape(N, 128, 2048).astype(BF), rng)
    return {"wc": c, "ws": s}
def setup_inputs(rng):
    return {**numbers_of(rng), **lists(rng), **weights(rng)}
def setup_inputs_ties(rng):
    d = numbers_of(rng)
    x = d["x"].reshape(N, 8, 16, C, 4)
    k = rng.integers(0, 3, (N, 8, C))
    k[:, rng.permutation(8)[:3]] = 1
    x[:, :, 0] = 0
    x[:, :, 0, :, 0] = k.astype(np.float32).astype(BF)
    z = (N, 8, 8, C, 4)
    odd = (1 + (2 * rng.integers(0, 64, z) + 1) * 2.0 ** -7) * np.exp2(-1.0 * rng.integers(8, 15, z)) * rng.choice([-1.0, 1.0], z)
    odd[:, :, 0, :, 0] = 1.96875
    o = rng.permutation(N)
    odd[o[2], :, 0, :, 1] = rng.integers(2, 32, (8, C)) * 2.0 ** -17
    x[:, :, 8:] = odd.astype(np.float32).astype(BF)
    u = d["u"].reshape(N, 128, 128, 4)
    u[:, :, ::16] = 0
    for r in range(N):
        for h in range(0, 128, 16):
            if r == o[2]: u[r, h + 8, h, 1] = 1.0
            else: u[r, h, h, 0] = 0.0 if r == o[0] else -1.0 if r == o[1] else 1.0
    l = lists(rng)
    t = np.array(gentries(l["p"][o[0]]))
    t[:, rng.permutation(J)[:J // 4]] = C - 32 + 4 * rng.integers(0, 8, (1, J // 4)) + np.arange(8)[:, None] % 2
    l["p"][o[0]] = gtable(t)
    return {"x": x.reshape(N, 128, 4 * C), "u": u.reshape(N, 128, 512), "v": d["v"], **l, **weights(rng, [0])}
def setup_inputs_near(rng):
    d = numbers_of(rng)
    x = d["x"].astype(np.float32).reshape(N, 8, 16, C, 4)
    x[:, :, :2] = 0
    x[:, :, 2:8] *= np.float32(0.25)
    x[:, :, 8:] = 0
    x[:, :, 0, :, 0] = 1
    x[:, :, 1, :, 0] = 2.0 ** -10
    s = rng.integers(0, 16, (N, 8, C))
    x[:, :, 8] = ((s[:, :, :, None] >> np.arange(4)) & 1) * np.exp2(np.arange(4) - 24.0)
    x[:, :, 10, :, 0] = (1 + 0.125 * rng.integers(0, 8, (N, 8, C))) * 2.0 ** -30
    x[:, :, 12] = x[:, :, 10]
    u = d["u"].reshape(N, 128, 128, 4)
    u[:, :, ::16] = 0
    o = rng.permutation(N) % 4
    for r in range(N):
        k = 2.0 ** -30 if o[r] in (1, 3) else 1.0
        sign = rng.permutation(8) % 2 * 2.0 - 1.0
        for g in range(8):
            h = 16 * g
            if o[r] == 3:
                u[r, h + 10, h, 0] = 1.125 * k * sign[g]
                u[r, h + 12, h, 0] = -k * sign[g]
            else:
                u[r, h, h, 0] = -k if o[r] == 2 else k
                u[r, h + 1, h, 0] = k
                u[r, h + 8, h] = 2 * k
    return {"x": x.reshape(N, 128, 4 * C).astype(BF), "u": u.reshape(N, 128, 512), "v": d["v"], **lists(rng), **weights(rng, [0, 1, 8, 9, 10, 11, 12, 13, 14, 15])}
def setup_inputs_huge(rng):
    d = numbers_of(rng)
    h = rng.permutation(8)
    x = -0.95 - 0.05 * rng.random((N, 8, 16, C, 4))
    x[:, h[4:]] = (0.75 + 0.1 * rng.random((N, 4, 16, C, 4))) * rng.choice([-1.0, 1.0], (N, 4, 1, C, 1))
    u = d["u"].reshape(N, 128, 128, 4)
    u[:, :, ::16] = 0
    for r in range(N):
        below = rng.permutation(8) < 4
        for g in range(8):
            a = 16 * int(rng.choice(h[:4] if below[g] else h[4:]))
            u[r, a:a + 16, 16 * g] = (2.0 ** 30 * (1 - 0.1 * rng.random((16, 4)))).astype(np.float32).astype(BF)
    return {"x": (2.0 ** 30 * x).astype(np.float32).reshape(N, 128, 4 * C).astype(BF), "u": u.reshape(N, 128, 512), "v": d["v"], **lists(rng), **weights(rng)}
def setup_inputs_ends(rng):
    d = numbers_of(rng)
    o = rng.permutation(N)
    sign = rng.integers(0, 2, (8, 16, 1, 4)) * 2.0 - 1.0
    x = np.zeros((N, 8, 16, C, 4))
    u = d["u"].reshape(N, 128, 128, 4)
    u[:, :, ::16] = 0
    v = np.zeros((N, 128, 512))
    n = rng.integers(0, C, (8, C))
    j = 1 + rng.permutation(C - 2)
    n[:, j[:C // 3]] = 0
    n[:, j[C // 3:2 * (C // 3)]] = C - 1
    t = np.stack([paths(rng, n) for r in range(N)])
    for i in range(N):
        r, k = o[i], 2.0 ** 30 if i % 2 == 0 else 2.0 ** -30
        if i % 2 == 0: x[r] = sign * k * (1 - 0.125 * rng.integers(0, 4, (8, 1, C, 1)))
        else: x[r] = sign * k * (1 + 0.125 * rng.integers(0, 8, (8, 1, C, 1)))
        none = 1 + rng.permutation(6)[:2]
        for g in range(8):
            if g in none: continue
            b = -1.0 if i == 0 else 1.0 if i == 2 else rng.choice([-1.0, 1.0])
            u[r, :, 16 * g] = (sign.reshape(128, 4) * (k * b)).astype(np.float32).astype(BF)
        v[r] = rng.choice([-1.0, 1.0], (128, 512)) * k
    t[o[0]] = C - 1
    t[o[1]] = 0
    t[o[2]] = np.where(np.arange(8) % 2 == 1, C - 1, 0)[:, None]
    return {"x": x.astype(np.float32).reshape(N, 128, 4 * C).astype(BF), "u": u.reshape(N, 128, 512), "v": v.astype(np.float32).astype(BF), "nb": np.stack([gtable(n)] * N), "p": np.stack([gtable(t[r]) for r in range(N)]), **weights(rng, range(16))}
def setup_inputs_spread(rng):
    d = setup_inputs(rng)
    d["x"] = big(wide(rng, N, 128, 4 * C, cols=6))
    return d
def check_inputs(d):
    b = []
    for k in ("x", "u", "v"):
        a = np.abs(d[k].astype(np.float32))
        if not (np.isfinite(a).all() and ((a == 0) | (a >= 2.0 ** -30) & (a <= 2.0 ** 30)).all()): b.append("a value of " + k)
    for k in ("nb", "p"):
        if not ((d[k] >= 0) & (d[k] < C)).all(): b.append("an entry of " + k)
    if (d["nb"] != d["nb"][:1]).any(): b.append("nb isn't the same on all ranks")
    none, least, most = [emit(mx_ref.quantize(np.full((128, 16), k, np.float32).astype(BF)))[1][0, 0] for k in (0.0, 2.0 ** -30, 2.0 ** 30)]
    tops = emit(mx_ref.quantize((np.ones((128, 1)) * np.repeat(1 + np.arange(128) * 2.0 ** -7, 4)).astype(np.float32).astype(BF)))[0] & 0x7F
    for r in range(N):
        if ((d["wc"][r] & 0x7F) == 0x7F).any(): b.append("wc: a code that is no number")
        s = mx_ref.live(d["ws"][r])
        if ((s != none) & ((s < least) | (s > most))).any(): b.append("ws: a scale out of range")
        elif not (np.sum(np.abs(decode(pk(d["wc"][r], d["ws"][r])).astype(np.float64)).reshape(128, 512, 4), axis=(0, 2)) <= 32).all(): b.append("the sizes in a column of W")
        a = np.max((d["wc"][r] & 0x7F).reshape(16, 8, 512, 4), axis=(1, 3))
        if not np.where(s == none, a == 0, (a >= np.min(tops)) & (a <= np.max(tops))).all(): b.append("wc: the codes of a block")
    return b
def hop(a, s, n):
    a = np.array(a)
    best = [n[np.argmax(s[e][n], axis=0), np.arange(C)] for e in (0, 7)]
    for h in range(4):
        for g in range(h % 2, 8, 2):
            if g == 0 or g == 7:
                m = a[1] if g == 0 else a[6]
                b = np.where(a[g] == m, best[0 if g == 0 else 1][m], m)
            else:
                low, high = a[g - 1] == a[g], a[g + 1] == a[g]
                b = np.where(low & ~high, a[g + 1], np.where(high & ~low, a[g - 1], a[g]))
            a[g] = np.where(s[g][b] > s[g][a[g]], b, a[g])
    return a
def reference(x, u, v, nb, p, wc, ws):
    qu = [mx_ref.quantize(u[r]) for r in range(N)]
    lay = [pk(wc[r], ws[r]) for r in range(N)]
    now = [x[r] for r in range(N)]
    at = [gentries(p[r]) for r in range(N)]
    for t in range(R):
        have, moved, z, first, gone = [], [], [], [], []
        for r in range(N):
            q = mx_ref.quantize(now[r])
            have.append(decode(q).astype(BF))
            s = mx_ref.matmul(qu[r], q)[::16] + np.float32(0.0)
            a = hop(at[r], s, gentries(nb[r]))
            bond = np.concatenate([a[1:], a[6:7]])
            z.append(((gcols(have[r], a).astype(np.float32) + gcols(have[r], bond).astype(np.float32)) * np.float32(0.5)).astype(BF))
            first.append(np.argsort(-np.sum(a[:-1] != a[1:], axis=0), kind="stable")[:K])
            gone.append(mx_ref.quantize(np.ascontiguousarray(cols(z[r], first[r]))))
            moved.append(a)
        for r in range(N):
            e = (r - 1) % N
            l = tile([mx_ref.matmul(pick(lay[r], np.arange(128 * b, 128 * b + 128)), gone[e]) * np.float32(0.03125) for b in range(4)])
            y = np.array(z[r]).reshape(128, J, 4)
            y[:, first[r]] = l.reshape(128, K, 4)
            at[r] = np.array(moved[r])
            at[r][:, first[r]] = moved[e][:, first[e]]
            low = np.stack([J + np.arange(C)] * 8)
            np.minimum.at(low, (np.arange(8)[:, None], at[r]), np.arange(J)[None])
            w = gcols(np.concatenate([y.reshape(128, 4 * J), have[r]], axis=1), low)
            now[r] = ((have[r].astype(np.float32) + w.astype(np.float32)) * np.float32(0.5)).astype(BF)
    y, ad = np.zeros((N, 128, C), np.float32), np.zeros((N, 8, J), np.float32)
    oc, osc = np.zeros((N, 128, 4 * C), np.uint8), np.zeros((N, 16, C), np.uint8)
    for r in range(N):
        q = mx_ref.quantize(now[r])
        y[r] = mx_ref.matmul(mx_ref.quantize(v[r]), q)
        ad[r] = at[r]
        oc[r], osc[r] = emit(q)
    return {"y": y, "ad": ad, "oc": oc, "osc": osc}

from concourse.mybir import ActivationFunctionType, AluOpType, AxisListType, dt

ALU = AluOpType
ACT = ActivationFunctionType
N, C, J, K, R = 4, 288, 448, 160, 3
NSEG, SEG = 18, 450
S1 = 4096.0
POS = [8 + C * 7] + [8 + C * k for k in range(7)]
BAD = 8 + 10 * C
ADR = BAD + 8 - POS[7]
WIN = BAD + 8 + 4 * C
YW = J + K + C
VSEG, CUT = 8, 13

_SB = {
    "float32": {"idn": [608], "e512": [448], "exf": [4], "elf": [28], "t512": [8], "hi4": [18], "bas": [4, 8], "cdf": [8, 8], "kf": [160],
                "nbf": [32], "nx": [32], "sw": [WIN], "bg": [1024], "bsc": [1024], "b2": [8, 16], "m1": [8, 12], "m2": [8, 10], "m3": [8, 8],
                "cw": [8, 8], "k1": [8, 4], "k2": [8, 2], "k5": [4], "k6": [8], "xd": [32], "td": [32], "bl": [18], "tx": [32], "xt": [32],
                "xa": [4, 10], "eb": [4, 10], "ab": [4, 8], "sg": [512], "si": [512], "pr": [4, 4], "x1": [4, 4], "yy": [4, 4], "og": [4, 4],
                "mv": [4, 4], "t4": [4, 4], "hg": [320], "sk": [320], "sc0": [4, 4], "sc1": [4, 4], "ne": [4, 16], "d1": [4, 12], "d2": [4, 10],
                "d3": [4, 8], "q1": [4, 8], "q2": [4, 8], "q3": [4, 8], "xp": [32], "tp": [32], "kx": [4], "kn": [4], "lc": [28], "kr": [448],
                "ac": [4], "pl": [28], "apk": [448], "sr": [448], "sdm": [160], "sds": [160], "ls": [10], "kpf": [28], "ka": [28], "kb": [28], "lx": [28],
                "srct": [472], "la": [32], "ar": [176], "ln": [28], "jm": [18], "ysb": [288]},
    "bfloat16": {"mk": [512], "rst": [512], "tabh": [304], "one": [8 * SEG], "ut": [512], "vt": [512], "mt": [4 * C], "at": [4 * K], "eo": [512],
                 "et": [2048], "jk": [448], "oh": [448], "fq": [4 * C], "fh": [4 * C], "gq": [4 * J], "yf": [4 * YW], "nd": [NSEG * SEG], "hr": [SEG],
                 "w2": [176]},
    "float16": {"jb": [NSEG * SEG], "ng": [448], "ns": [448], "fg": [288], "fs": [288]},
    "int32": {"ki": [512], "kj": [512], "ku": [64], "kp": [28], "kq": [4], "pi": [28], "nbt": [32], "bli": [18], "blj": [18], "blk": [18],
              "ci": [28], "ai": [28], "di": [28], "bi": [28], "fi": [10], "fj": [10]},
    "uint16": {"rv16": [28], "ul16": [64], "bo16": [32], "p16": [28], "b016": [18], "b716": [18], "of16": [32], "o16": [20], "a16": [28], "d16": [28],
               "b16": [28], "pos16": [28], "f16": [10], "pcs": [28], "kl16": [28], "src16": [28], "aa16": [10], "j16": [18], "fl16": [18], "nl16": [28]},
    "float8_e4m3fn_x4": {"uq": [128], "uqr": [1024], "vq": [128], "wq": [512], "mq": [C], "aq": [K], "ca": [3 * K], "eq": [512]},
    "uint8": {"us": [128], "usr": [1024], "vs": [128], "wsp": [512], "ms": [C], "asc": [K], "sa": [3 * K], "es": [512]},
}
_WHOLE = ("rv16 ul16 bo16 p16 b016 b716 of16 a16 d16 b16 pos16 f16 pcs kl16 src16 aa16 j16 fl16 nl16 exf elf hi4 kpf ka kb lx jm k5 "
          "bli blj blk ci ai fi fj kq").split()
_SMALL = {"uint16": "lu", "float32": "lf", "int32": "li"}
_SIDE = {d: [n for n in _SB[d] if n in _WHOLE] for d in _SMALL}
SCRATCH = {n: ("sbuf", [128] + s, d) for d, b in _SB.items() for n, s in b.items() if n not in _SIDE.get(d, [])}
SCRATCH.update({_SMALL[d]: ("sbuf", [128, sum(32 * ((_SB[d][n][0] + 31) // 32) for n in b)], d) for d, b in _SIDE.items()})
SCRATCH["ps"] = ("psum", [128, 4096], "float32")
SEMAPHORES = (["qv", "qa", "qt", "qg", "dx", "du", "dp", "dn", "dw", "dv", "dtab", "dl1", "dl2", "dst", "dout", "lls", "lca"]
              + ["r%s%d" % (k, t) for k in "lc" for t in range(R)])


def rank_program(g, core, T, topo):
    rank = T.rank_of(core)
    if rank is None:
        return
    B = {n: T[n] for n in SCRATCH}
    for d, b in _SIDE.items():
        pos = 0
        for n in b:
            B[n] = {slice(None): T[_SMALL[d]][:, pos:pos + _SB[d][n][0]]}
            pos += 32 * ((_SB[d][n][0] + 31) // 32)
    ENG = {"v": g.vector, "a": g.scalar, "t": g.tensor, "g": g, "s": g.sync}
    cnt = {s: 0 for s in SEMAPHORES}
    seen, lastw, reads = {}, {}, {}

    def wait(q, sem, val):
        if seen.get((q, sem), 0) < val:
            ENG[q].wait_ge(T.sem[sem], val)
            seen[(q, sem)] = val

    def need(q, rd, wr):
        for k in rd + wr:
            if k in lastw:
                wait(q, *lastw[k])
        for k in wr:
            for sem, val in reads.get(k, {}).items():
                wait(q, sem, val)

    def done(rd, wr, sem):
        for k in rd:
            reads.setdefault(k, {})[sem] = cnt[sem]
        for k in wr:
            lastw[k] = (sem, cnt[sem])
            reads[k] = {}

    def op(q, rd, wr, f):
        rd, wr, sem = rd.split(), wr.split(), "q" + q
        need(q, rd, wr)
        f(ENG[q]).then_inc(T.sem[sem], 1)
        cnt[sem] += 1
        done(rd, wr, sem)

    def dma(sem, rd, wr, moves, queues="s"):
        rd, wr = rd.split(), wr.split()
        for i, q in enumerate(queues):
            need(q, rd, wr)
            for o, a in moves[i::len(queues)]:
                ENG[q].dma_start(o, a).then_inc(T.sem[sem], 16)
                cnt[sem] += 16
        done(rd, wr, sem)

    def cp(o, i, rd, wr):
        op("v", rd, wr, lambda e: e.tensor_copy(o, i))

    def tt(o, a, b, f, rd, wr):
        op("v", rd, wr, lambda e: e.tensor_tensor(o, a, b, f))

    def ts(o, a, s1, f1, rd, wr, s2=None, f2=None):
        if f2 is None:
            op("v", rd, wr, lambda e: e.tensor_scalar(o, a, s1, None, f1))
        else:
            op("v", rd, wr, lambda e: e.tensor_scalar(o, a, s1, s2, f1, f2))

    def fill(o, c, wr):
        op("v", "", wr, lambda e: e.memset(o, c))

    def scan(o, a, b, init, f1, f2, rd, wr):
        op("v", rd, wr, lambda e: e.tensor_tensor_scan(o, a, b, init, f1, f2))

    def own16(o, m, n, rd, wr):
        scan(o, B["rst"][:, 0:n], m, 0.0, ALU.mult, ALU.add, rd + " rst", wr)

    def act(o, i, rd, wr, func=ACT.Copy, **kw):
        op("a", rd, wr, lambda e: e.activation(o, i, func, **kw))

    def turn(o, i, rd, wr):
        op("v", rd, wr, lambda e: e.transpose(o, i))

    def quant(o, s, i, rd, wr):
        op("v", rd, wr, lambda e: e.quantize_mx(o, s, i))

    def mm(b, n, l, ls, r, rs, rd):
        op("t", rd, PS[b], lambda e: e.matmul_mx(bank(b, n), l, ls, r, rs, True, True))

    def iota(o, pat, base, cm, wr, fl=False):
        if fl:
            op("g", "", wr, lambda e: e.iota(o, pat, base, cm, allow_small_or_imprecise_dtypes=True))
        else:
            op("g", "", wr, lambda e: e.iota(o, pat, base, cm))

    def bank(b, n):
        return B["ps"][:, 512 * b:512 * b + n]

    PS = ["ps%d" % b for b in range(8)]
    MT = "mt0 mt1 mt2 mt3"
    idn, mk, sw, yf, kf = B["idn"], B["mk"], B["sw"], B["yf"], B["kf"]
    nxt, prv = T.cores[(rank + 1) % N], T.cores[(rank - 1) % N]
    rid, pid, _ = topo.addr(nxt)
    mask, n_out, n_in = topo.mask(core, nxt), len(topo.engines(core, nxt)), len(topo.engines(prv, core))

    def send(rd, lsem, rsem, moves):
        need("g", [rd], [])
        for o, i in moves:
            g.remote_dma(out_ap=o, in_ap=i, remote_sem=T.sem[rsem], local_sem=T.sem[lsem], pid=pid, routing_id=rid, dma_engine_mask=mask)
            cnt[lsem] += n_out
        done([rd], [], lsem)

    fill(B["tx"][:], 0.0, "tx")
    fill(B["nbt"][:], 0, "nbt")
    dma("dx", "", MT, [(B["mt"][:], T.x[:])])
    dma("du", "", "ut", [(B["ut"][:], T.u[:])], "a")
    dma("dp", "", "pi", [(B["pi"][:], T.p[:])])
    dma("dn", "", "nbt", [(B["nbt"][t:128:8, 0:18], T.nb[16 * t:16 * t + 16, :]) for t in range(8)], "as")
    dma("dw", "", "wq wsp", [(B["wq"][:].bitcast(dt.uint8), T.wc[:]), (B["wsp"][:], T.ws[:])])
    dma("dv", "", "vt", [(B["vt"][:], T.v[:])])

    iota(B["ku"][:], [[16, 8], [0, 8]], 0, 0, "ku")
    iota(B["kj"][:], [[1, 512]], 128, -1, "kj")
    iota(B["kp"][:], [[0, 28]], 0, 1, "kp")
    iota(kf[:, 96:124], [[16, 28]], 0, 0, "kfc", True)
    iota(idn[:], [[1, 608]], 0, 0, "idn", True)
    iota(B["ki"][:], [[1, 512]], 0, 0, "ki")
    iota(kf[:, 32:96], [[0, 8], [-512, 8]], 3584, 0, "kfb", True)
    iota(kf[:, 0:32], [[0, 4], [C, 8]], POS[1] - C, 0, "kfa", True)
    iota(B["kq"][:], [[0, 4]], 0, 1, "kq")
    iota(kf[:, 128:146], [[-16, 18]], YW - C + 16 * 17, 0, "kfd", True)
    fill(B["eo"][:], 1.0, "eo")
    for b in range(4):
        op("g", "eo", "et%d" % b, lambda e: e.affine_select(B["et"][:, 512 * b:512 * b + 512], B["eo"][:], [[1, 512]], ALU.is_equal, 0.0, -b, -4))
    iota(B["one"][:], [[0, 8 * SEG]], 1, 0, "one", True)
    cp(B["ul16"][:], B["ku"][:], "ku", "ul16")
    ts(B["kj"][:], B["kj"][:], 15, ALU.bitwise_and, "kj", "kj")
    ts(mk[:], B["kj"][:], 0.0, ALU.is_equal, "kj", "mk")
    ts(B["kp"][:], B["kp"][:], 15, ALU.bitwise_and, "kp", "kp")
    tt(B["elf"][:], kf[:, 96:124], B["kp"][:], ALU.add, "kfc kp", "elf")
    ts(B["rv16"][:], B["elf"][:], -1.0, ALU.mult, "elf", "rv16", float(J - 1), ALU.add)
    quant(B["uq"][:], B["us"][:], B["ut"][:], "ut", "uq")
    cp(B["uqr"][:].bitcast(dt.uint32), B["uq"][:].bitcast(dt.uint32).indirect(B["ul16"][:]), "uq ul16", "uqr")
    act(B["usr"][:], B["us"][:].indirect(B["ul16"][:]), "uq ul16", "usr")
    quant(B["mq"][:], B["ms"][:], B["mt"][:], MT, "mq")
    for k in (7, 0):
        act(sw[:, ADR + POS[k]:ADR + POS[k] + C], idn[:, 0:C], "idn", "swi%d" % k, scale=S1)
    act(B["e512"][:], idn[:, 0:J], "idn", "e512", scale=512.0)
    act(B["t512"][:], idn[:, 0:8], "idn", "t512", scale=512.0)
    cp(B["p16"][:], B["pi"][:], "pi", "p16")
    cp(B["kr"][:], idn[:, 0:C].indirect(B["p16"][:]), "idn p16", "kr")
    ts(B["kj"][:], B["ki"][:], 15, ALU.bitwise_and, "ki", "kj")
    ts(B["rst"][:], B["kj"][:], 0.0, ALU.not_equal, "kj", "rst")
    tt(B["ng"][:], B["kr"][:].indirect(B["rv16"][:]), mk[:, 0:J], ALU.mult, "kr rv16 mk", "ng")
    own16(B["ns"][:], B["ng"][:], J, "ng", "ns")
    cp(B["ln"][:], B["ns"][:, 15:J:16], "ns", "ln")

    def to_x():
        dma("dst", "ln", "tx", [(B["tx"][k:128:8, 0:28], B["ln"][16 * k:16 * k + 16, :]) for k in range(8)])
    to_x()
    cp(B["nbf"][:], B["nbt"][:], "nbt", "nbf")
    turn(B["nx"][:], B["nbf"][:], "nbf", "nx")
    cp(B["bo16"][:], B["nx"][:], "nx", "bo16")
    for k in (0, 4):
        tt(B["cdf"][:, k:k + 4, :], kf[:, 32:64], B["nx"][:], ALU.add, "kfb nx", "cdf%d" % k)
    fill(B["xd"][:], 0.0, "xd")

    def const_hops():
        fill(B["eb"][:], 0.0, "eb")
        fill(B["xa"][:], 0.0, "xa")
        ts(B["bas"][:], kf[:, 0:32], S1, ALU.mult, "kfa", "bas")
        fill(B["bas"][:, :, 0], POS[0] * S1, "bas")
        quant(B["eq"][:], B["es"][:], B["et"][:], "et0 et1 et2 et3", "eq")
        fill(sw[:, 0:8], -1e29, "swc0")
        fill(sw[:, BAD:BAD + 8], -1e29, "swc1")

    def const_rows():
        ts(B["di"][:, 0:4], B["kq"][:], 31, ALU.bitwise_and, "kq", "di")
        ts(B["bi"][:, 0:4], B["kq"][:], 5, ALU.arith_shift_right, "kq", "bi")
        ts(B["kx"][:], B["di"][:, 0:4], 16.0, ALU.mult, "di", "kx")
        ts(B["kn"][:], B["bi"][:, 0:4], 4.0, ALU.mult, "bi", "kn")
        tt(B["exf"][:], B["kx"][:], B["kn"][:], ALU.add, "kx kn", "exf")
        tt(B["exf"][:], B["exf"][:], idn[:, 0:4], ALU.add, "exf idn", "exf")
        hi = B["sg"]
        ts(B["kj"][:, 0:C], B["ki"][:, 0:C], 4, ALU.arith_shift_right, "ki", "kj")
        ts(hi[:, 0:C], B["kj"][:, 0:C], -64.0, ALU.add, "kj", "sg")
        tt(hi[:, 0:C], hi[:, 0:C], mk[:, 0:C], ALU.mult, "sg mk", "sg")
        ts(B["tabh"][:, 0:C], hi[:, 0:C], 64.0, ALU.add, "sg", "tabh")
        fill(B["tabh"][:, C:304], 0.0, "tabh2")
        tt(B["srct"][:, 0:NSEG], kf[:, 128:146], B["kp"][:, 0:NSEG], ALU.add, "kfd kp", "srcc")
        fill(B["w2"][:, K:176], 0.0, "w20")
        fill(B["hr"][:, 0:2], 64.0, "hr0")
        fill(B["ar"][:, K:176], 0.0, "ar0")
        ts(B["hi4"][:], idn[:, 0:NSEG], 449.0, ALU.add, "idn", "hi4")
        quant(B["vq"][:], B["vs"][:], B["vt"][:], "vt", "vq")
        fill(B["one"][:, 0:8 * SEG:SEG], 1000.0, "one")

    def next_chains():
        cp(B["ar"][:, 0:K], idn[:, 0:C].indirect(B["aa16"][:]), "idn aa16", "ar")
        tt(B["ng"][:], B["ar"][:].indirect(B["pcs"][:]), mk[:, 0:J], ALU.mult, "ar ar0 pcs mk", "ng")
        own16(B["ns"][:], B["ng"][:], J, "ng", "ns")
        tt(B["ln"][:], B["ns"][:, 15:J:16], B["kb"][:], ALU.add, "ns kb", "ln")

    for t in range(R):
        for k in (0, 7, 2, 4, 6, 1, 3, 5):
            mm(k, C, B["uqr"][:, 128 * k:128 * k + 128], B["usr"][:, 128 * k:128 * k + 128], B["mq"][:], B["ms"][:], "uqr usr mq")
        if t:
            next_chains()
            to_x()
        for k in (0, 7, 2, 4, 6, 1, 3, 5):
            o = sw[:, POS[k]:POS[k] + C]
            if k == 0 and t == 0:
                cp(o, bank(k, C), PS[k], "s0")
            else:
                act(o, bank(k, C), PS[k], "s%d" % k)
        SC = " ".join("s%d" % k for k in range(8))
        for i, k in enumerate((0, 7)):
            tt(B["bg"][:, 512 * i:512 * i + 512], sw[:, POS[k]:POS[k] + C].indirect(B["bo16"][:]), mk[:], ALU.mult, "s%d bo16 mk" % k, "bg%d" % i)
        for i in (0, 1):
            own16(B["bsc"][:, 512 * i:512 * i + 512], B["bg"][:, 512 * i:512 * i + 512], 512, "bg%d" % i, "bsc%d" % i)
        b2, m1, m2, m3 = B["b2"], B["m1"], B["m2"], B["m3"]
        for i in (0, 8):
            cp(b2[:, :, i:i + 8], B["bsc"][:, 15:1024:16], "bsc0 bsc1", "b2%d" % i)
        tt(m1[:], b2[:, :, 0:12], b2[:, :, 4:16], ALU.max, "b20 b28", "m1")
        tt(m2[:], m1[:, :, 0:10], m1[:, :, 2:12], ALU.max, "m1", "m2")
        tt(m3[:], m2[:, :, 0:8], m2[:, :, 1:9], ALU.max, "m2", "m3")
        tt(B["cw"][:], b2[:, :, 0:8], m3[:], ALU.is_equal, "b20 m3", "cw")
        tt(B["cw"][:], B["cw"][:], B["cdf"][:], ALU.mult, "cw cdf0 cdf4", "cw")
        tt(B["k1"][:], B["cw"][:, :, 0:4], B["cw"][:, :, 4:8], ALU.max, "cw", "k1")
        tt(B["k2"][:], B["k1"][:, :, 0:2], B["k1"][:, :, 2:4], ALU.max, "k1", "k2")
        tt(B["k6"][:], B["k2"][:, :, 0], B["k2"][:, :, 1], ALU.max, "k2", "k6")
        ts(B["k5"][:], B["k6"][:, 4:8], 4096.0, ALU.mult, "k6", "k5")
        tt(B["xd"][:, 0:32:8], B["k5"][:], B["k6"][:, 0:4], ALU.add, "k5 k6", "xd")
        turn(B["td"][:], B["xd"][:], "xd", "td")
        dma("dtab", "td", "bl", [(B["bl"][16 * k:16 * k + 16, :], B["td"][0:128:8, 0:18]) for k in range(8)], "sa")
        if t == 0:
            const_hops()
        xa, eb, ab = B["xa"], B["eb"], B["ab"]
        turn(B["xt"][:], B["tx"][:], "tx", "xt")
        ts(xa[:, :, 1:9], B["xt"][:], S1, ALU.mult, "xt", "xa")
        tt(ab[:], xa[:, :, 1:9], B["bas"][:], ALU.add, "xa bas", "ab")
        ts(B["of16"][:], ab[:], 1.0 / S1, ALU.mult, "ab", "of16")
        tt(B["sg"][:], sw[:, 0:8 + 8 * C].indirect(B["of16"][:]), mk[:], ALU.mult, SC + " swc0 of16 mk", "sg")
        own16(B["si"][:], B["sg"][:], 512, "sg", "si")
        cp(B["bli"][:], B["bl"][:], "bl", "bli")
        ts(B["blj"][:], B["bli"][:], 511, ALU.bitwise_and, "bli", "blj")
        ts(B["blk"][:], B["bli"][:], 12, ALU.arith_shift_right, "bli", "blk", 511, ALU.bitwise_and)
        cp(B["b016"][:], B["blj"][:], "blj", "b016")
        cp(B["b716"][:], B["blk"][:], "blk", "b716")
        for k in (0, 7):
            l, o = B["b%d16" % k][:], POS[k] + 2 * C
            if k == 0:
                cp(sw[:, o:o + C], sw[:, POS[k]:POS[k] + C].indirect(l), "s0 b016", "bs0")
            else:
                act(sw[:, o:o + C], sw[:, POS[k]:POS[k] + C].indirect(l), "s7 b716", "bs7")
            act(sw[:, ADR + o:ADR + o + C], idn[:, 0:C].indirect(l), "idn b%d16" % k, "db%d" % k, scale=S1)
        for b in range(4):
            mm(b, C, B["eq"][:, 128 * b:128 * b + 128], B["es"][:, 128 * b:128 * b + 128], B["mq"][:], B["ms"][:], "eq mq")
            act(B["fq"][:, C * b:C * b + C], bank(b, C), PS[b], "fq%d" % b, scale=0.25)
            act(yf[:, YW * b + J + K:YW * b + YW], bank(b, C), PS[b], "yf%d" % b, scale=0.5)
            act(B["fh"][:, C * b:C * b + C], bank(b, C), PS[b], "fh%d" % b, scale=0.5)
        ALLW = SC + " swc0 swc1 swi0 swi7 bs0 bs7 db0 db7 "
        x1, pr, mv, sk = B["x1"], B["pr"], B["mv"], B["sk"]
        for h in range(4):
            par = h % 2
            sp, lk = (0, 1) if par == 0 else (3, 7)
            lo, up = eb[:, :, par:7 + par:2], eb[:, :, 1 + par:8 + par:2]
            tt(eb[:, :, 1:8], xa[:, :, 2:9], xa[:, :, 1:8], ALU.subtract, "xa", "eb")
            tt(pr[:], up, lo, ALU.mult, "eb", "pr")
            tt(x1[:], up, lo, ALU.subtract, "eb", "x1")
            ts(pr[:, :, sp], eb[:, :, lk], 0.0, ALU.is_equal, "eb pr", "pr", 2 * C * S1, ALU.mult)
            tt(B["yy"][:], x1[:], ab[:, :, par:8:2], ALU.add, "x1 ab", "yy")
            tt(B["og"][:], B["yy"][:], pr[:], ALU.add, "yy pr", "og")
            ts(B["o16"][:, 0:16], B["og"][:], 1.0 / S1, ALU.mult, "og", "o16a", float(BAD), ALU.min)
            ts(B["o16"][:, 16:20], B["og"][:, :, sp], 1.0 / S1, ALU.mult, "og", "o16b", float(ADR), ALU.add)
            tt(B["hg"][:], sw[:].indirect(B["o16"][:]), mk[:, 0:320], ALU.mult, ALLW + "o16a o16b mk", "hg")
            own16(sk[:], B["hg"][:], 320, "hg", "sk")
            mine = B["si"][:, 15 + 16 * par:512:32] if h < 2 else B["sc%d" % par][:]
            tt(mv[:], sk[:, 15:256:16], mine, ALU.is_gt, "sk si sc%d" % par, "mv")
            tt(x1[:, :, sp], sk[:, 271:320:16], xa[:, :, 1 + 7 * par], ALU.subtract, "sk xa x1", "x1")
            tt(B["t4"][:], mv[:], x1[:], ALU.mult, "mv x1", "t4")
            tt(xa[:, :, 1 + par:9:2], xa[:, :, 1 + par:9:2], B["t4"][:], ALU.add, "xa t4", "xa")
            if h < 2:
                tt(ab[:, :, par:8:2], ab[:, :, par:8:2], B["t4"][:], ALU.add, "ab t4", "ab")
                tt(B["sc%d" % par][:], sk[:, 15:256:16], mine, ALU.max, "sk si", "sc%d" % par)
        ne, d1, d2, d3 = B["ne"], B["d1"], B["d2"], B["d3"]
        tt(eb[:, :, 1:8], xa[:, :, 2:9], xa[:, :, 1:8], ALU.subtract, "xa", "eb")
        cp(xa[:, :, 9], xa[:, :, 7], "xa", "xa9")
        for i in (0, 8):
            ts(ne[:, :, i:i + 8], eb[:, :, 1:9], 0.0, ALU.not_equal, "eb", "ne%d" % i)
        ts(B["q1"][:], xa[:, :, 2:10], 512.0, ALU.mult, "xa xa9", "q1")
        tt(d1[:], ne[:, :, 0:12], ne[:, :, 4:16], ALU.add, "ne0 ne8", "d1")
        tt(B["q2"][:], B["q1"][:], xa[:, :, 1:9], ALU.add, "q1 xa", "q2")
        tt(d2[:], d1[:, :, 0:10], d1[:, :, 2:12], ALU.add, "d1", "d2")
        tt(d3[:], d2[:, :, 0:8], d2[:, :, 1:9], ALU.add, "d2", "d3")
        ts(B["q3"][:], d3[:], S1 * 2 ** 18, ALU.mult, "d3", "q3")
        tt(B["xp"][:], B["q2"][:], B["q3"][:], ALU.add, "q2 q3", "xp")
        turn(B["tp"][:], B["xp"][:], "xp", "tp")
        dma("dl1", "tp", "lc", [(B["lc"][16 * k:16 * k + 16, :], B["tp"][k:128:8, 0:28]) for k in range(8)], "sa")
        if t == 0:
            const_rows()
        ts(B["kx"][:], d3[:, :, 0], 512.0, ALU.mult, "d3", "kx")
        tt(B["kx"][:], B["kx"][:], B["exf"][:], ALU.add, "kx exf", "kx")
        ts(B["kn"][:], B["kx"][:], -1.0, ALU.mult, "kx", "kn")
        ts(B["ci"][:], B["lc"][:], 1.0 / S1, ALU.mult, "lc", "ci")
        ts(B["di"][:], B["ci"][:], 18, ALU.arith_shift_right, "ci", "di")
        ts(B["ai"][:], B["ci"][:], 511, ALU.bitwise_and, "ci", "ai")
        ts(B["bi"][:], B["ci"][:], 9, ALU.arith_shift_right, "ci", "bi", 511, ALU.bitwise_and)
        cp(B["d16"][:], B["di"][:], "di", "d16")
        cp(B["a16"][:], B["ai"][:], "ai", "a16")
        tt(B["kr"][:], B["t512"][:].indirect(B["d16"][:]), idn[:, 0:J], ALU.add, "t512 d16 idn", "kr")
        fq, gq, ac = B["fq"], B["gq"], B["ac"]

        def pick_f(b):
            act(gq[:, J * b:J * b + J], fq[:, C * b:C * b + C].indirect(B["a16"][:]), "fq%d a16" % b, "gq%d" % b)

        def bonds(b):
            tt(yf[:, YW * b:YW * b + J], fq[:, C * b:C * b + C].indirect(B["b16"][:]), gq[:, J * b:J * b + J], ALU.add, "fq%d b16 gq%d" % (b, b), "yz%d" % b)
        pick_f(0)
        for q in range(3):
            act(B["jk"][:], B["kr"][:], "kr kn", "jk ac%d" % q, ACT.Sign, bias=B["kn"][:, q:q + 1], accum_out=ac[:, q:q + 1])
        for b in (1, 2, 3):
            pick_f(b)
        cp(B["b16"][:], B["bi"][:], "bi", "b16")
        ts(B["sr"][:], B["kr"][:], B["kx"][:, 3:4], ALU.is_gt, "kr kx", "sr")
        op("v", "sr", "xd3", lambda e: e.tensor_reduce(B["xd"][:, 24:25], B["sr"][:], AxisListType.X, ALU.add))
        tt(B["apk"][:], idn[:, 0:C].indirect(B["a16"][:]), B["e512"][:], ALU.add, "idn a16 e512", "apk")
        ts(B["xd"][:, 0:24:8], ac[:, 0:3], 0.5, ALU.mult, "ac0 ac1 ac2 xd3", "xd", (J - 1) / 2.0, ALU.add)
        turn(B["td"][:], B["xd"][:], "xd", "td")
        dma("dl2", "td", "pl", [(B["pl"][16 * k:16 * k + 16, :], B["td"][0:128:8, 0:28]) for k in range(8)])
        for b in range(3):
            bonds(b)
        cp(B["pos16"][:], B["pl"][:], "pl", "pos16")
        cp(B["sr"][:].indirect(B["pos16"][:]), B["apk"][:], "apk pos16", "sr")
        tt(B["sdm"][:], B["sr"][:, 0:K], mk[:, 0:K], ALU.mult, "sr mk", "sdm")
        own16(B["sds"][:], B["sdm"][:], K, "sdm", "sds")
        cp(B["ls"][:], B["sds"][:, 15:K:16], "sds", "ls")
        send("ls", "lls", "rl%d" % t, [(B["la"][:, 10 * t:10 * t + 10], B["ls"][:])])
        kpf, lx = B["kpf"], B["lx"]
        cp(B["fi"][:], B["ls"][:], "ls", "fi")
        ts(kpf[:], B["pl"][:], float(K), ALU.is_ge, "pl", "kpf")
        ts(B["fj"][:], B["fi"][:], 9, ALU.arith_shift_right, "fi", "fj")
        ts(lx[:], B["ai"][:], -float(C), ALU.add, "ai", "lx")
        cp(B["f16"][:], B["fj"][:], "fj", "f16")
        tt(lx[:], lx[:], kpf[:], ALU.mult, "lx kpf", "lx")
        ts(B["pcs"][:], B["pl"][:], float(K), ALU.min, "pl", "pcs")
        ts(B["kl16"][:], lx[:], float(C), ALU.add, "lx", "kl16")
        bonds(3)
        at = B["at"]
        act(B["oh"][:], B["tabh"][:].indirect(B["kl16"][:]), "tabh tabh2 kl16", "oh")
        for b in range(4):
            act(at[:, b:4 * K:4], yf[:, YW * b:YW * b + J].indirect(B["f16"][:]), "yz%d f16" % b, "at%d" % b, scale=2.0)
        ts(B["ka"][:], B["pl"][:], float(K), ALU.is_lt, "pl", "ka")
        tt(lx[:], B["pl"][:], B["elf"][:], ALU.subtract, "pl elf", "lx")
        tt(B["kb"][:], kpf[:], B["ai"][:], ALU.mult, "kpf ai", "kb")
        ts(lx[:], lx[:], float(J), ALU.add, "lx", "lx")
        tt(lx[:], lx[:], B["ka"][:], ALU.mult, "lx ka", "lx")
        tt(lx[:], lx[:], B["elf"][:], ALU.add, "lx elf", "lx")
        cp(B["src16"][:], lx[:], "lx", "src16")
        cnt["rl%d" % t] = n_in
        lastw["la%d" % t] = ("rl%d" % t, n_in)
        cp(B["fi"][:], B["la"][:, 10 * t:10 * t + 10], "la%d" % t, "fi")
        ts(B["fj"][:], B["fi"][:], 511, ALU.bitwise_and, "fi", "fj")
        cp(B["aa16"][:], B["fj"][:], "fj", "aa16")
        cp(B["w2"][:, 0:K], B["tabh"][:].indirect(B["aa16"][:]), "tabh tabh2 aa16", "w2")
        hr, nd, jb = B["hr"], B["nd"], B["jb"]
        tt(hr[:, 2:SEG], B["w2"][:].indirect(B["pcs"][:]), B["oh"][:], ALU.add, "w2 w20 pcs oh", "hr")
        quant(B["aq"][:], B["asc"][:], at[:], "at0 at1 at2 at3", "aq")
        send("aq", "lca", "rc%d" % t, [(B["ca"][:, K * t:K * t + K].bitcast(dt.uint8), B["aq"][:].bitcast(dt.uint8)),
                                       (B["sa"][:, K * t:K * t + K], B["asc"][:])])
        for m in range(VSEG, NSEG):
            act(nd[:, SEG * m:SEG * m + SEG], hr[:], "hr hr0", "nd%d" % m, ACT.Abs, scale=2048.0, bias=-2048.0 * m)
        for m in range(VSEG):
            ts(nd[:, SEG * m:SEG * m + SEG], hr[:], float(m), ALU.not_equal, "hr hr0", "nd%d" % m, 2048.0, ALU.mult)

        def low(a, b):
            scan(jb[:, SEG * a:SEG * b], nd[:, SEG * a:SEG * b], B["one"][:, 0:SEG * (b - a)], 2000.0, ALU.min, ALU.add,
                 "one " + " ".join("nd%d" % m for m in range(a, b)), "jb%d" % a)
        low(0, VSEG)
        low(VSEG, CUT)
        act(B["srct"][:, NSEG:NSEG + J], idn[:].indirect(B["src16"][:]), "idn src16", "srct")
        cnt["rc%d" % t] = 2 * n_in
        lastw["ca%d" % t] = ("rc%d" % t, 2 * n_in)
        for b in range(4):
            mm(4 + b, K, B["wq"][:, 128 * b:128 * b + 128], B["wsp"][:, 128 * b:128 * b + 128], B["ca"][:, K * t:K * t + K], B["sa"][:, K * t:K * t + K], "wq wsp ca%d" % t)
            act(yf[:, YW * b + J:YW * b + J + K], bank(4 + b, K), PS[4 + b], "yl%d" % b, scale=2.0 ** -6)
        low(CUT, NSEG)
        tt(B["jm"][:], jb[:, SEG - 1:NSEG * SEG:SEG], B["hi4"][:], ALU.min, "jb0 jb%d jb%d hi4" % (VSEG, CUT), "jm")
        ts(B["j16"][:], B["jm"][:], -1.0, ALU.mult, "jm", "j16", float(J + NSEG), ALU.add)
        tt(B["fg"][:], B["srct"][:, 0:NSEG + J].indirect(B["j16"][:]), mk[:, 0:C], ALU.mult, "srcc srct j16 mk", "fg")
        own16(B["fs"][:], B["fg"][:], C, "fg", "fs")
        cp(B["fl16"][:], B["fs"][:, 15:C:16], "fs", "fl16")
        for b in range(4):
            tt(B["mt"][:, b:4 * C:4], yf[:, YW * b:YW * b + YW].indirect(B["fl16"][:]), B["fh"][:, C * b:C * b + C], ALU.add,
               "yz%d yl%d yf%d fh%d fl16" % (b, b, b, b), "mt%d" % b)
        quant(B["mq"][:], B["ms"][:], B["mt"][:], MT, "mq")

    dma("dout", "mq", "oc", [(T.oc[:], B["mq"][:].bitcast(dt.uint8))] + [(T.osc[4 * k:4 * k + 4, :], B["ms"][32 * k:32 * k + 4, :]) for k in range(4)])
    mm(0, C, B["vq"][:], B["vs"][:], B["mq"][:], B["ms"][:], "vq mq")
    act(B["ysb"][:], bank(0, C), PS[0], "ysb")
    dma("dout", "ysb", "y", [(T.y[:], B["ysb"][:])], "a")
    next_chains()
    cp(B["nl16"][:], B["ln"][:], "ln", "nl16")
    cp(B["kr"][:], idn[:, 0:C].indirect(B["nl16"][:]), "idn nl16", "kr")
    cp(B["apk"][:], B["kr"][:].indirect(B["rv16"][:]), "kr rv16", "apk")
    dma("dout", "apk", "ad", [(T.ad[:], B["apk"][0:128:16, :])])
    for s in SEMAPHORES:
        if cnt[s]:
            wait("g", s, cnt[s])
